import numpy as np
import ml_dtypes


def mxq(x, axis, fmt="e4m3"):
    dtype, down = {"e4m3": (ml_dtypes.float8_e4m3fn, 7), "e5m2": (ml_dtypes.float8_e5m2, 14)}[fmt]
    v = np.moveaxis(np.asarray(x, np.float32).astype(ml_dtypes.bfloat16).astype(np.float64), axis, -1)
    blocks = v.reshape(v.shape[:-1] + (-1, 32))
    amax = np.abs(blocks).max(-1, keepdims=True)
    byte = np.maximum(np.where(amax > 0, np.frexp(amax)[1] - 1 + 127, 0) - down, 1)
    scale = np.exp2(byte - 127.0)
    codes = (blocks / scale).astype(np.float32).astype(dtype).astype(np.float64)
    return np.moveaxis((codes * scale).reshape(v.shape), -1, axis)


WIDE = False


def mx_kscale(k):
    if not WIDE:
        return np.ones(k)
    levels = np.array([10, -10, 5, -5, 0])
    if k % 512:
        return np.exp2(np.random.permutation(np.resize(levels, k // 32))).repeat(32)
    a = np.empty((k // 512, 16))
    for p in range(k // 512):
        a[p, :8] = np.random.permutation(np.resize(levels, 8))
        for g in range(8):
            far = levels[np.abs(levels - a[p, g]) >= 10]
            a[p, g + 8] = far[np.random.randint(len(far))]
    return np.exp2(a.ravel()).repeat(32)


def f64(x):
    return np.asarray(x).astype(np.float64)


def striped8(idx):
    return np.asarray(idx).reshape(8, -1, 16).transpose(0, 2, 1).reshape(128, -1).astype(np.uint16)


def unstriped8(offs):
    return offs.reshape(8, 16, -1).transpose(0, 2, 1).reshape(8, -1).astype(np.int64)


def pick8(x, idx, run):
    r = np.arange(len(x))
    return x[r[:, None], idx[r % (8 * run) // run]]


E2M1 = np.array([0.0, 0.5, 1.0, 1.5, 2.0, 3.0, 4.0, 6.0, -0.0, -0.5, -1.0, -1.5, -2.0, -3.0, -4.0, -6.0])


def pack_weight(w, fmt):
    k, n = w.shape
    w = f64(np.asarray(w, np.float32).astype(ml_dtypes.bfloat16)).reshape(k // 32, 32, n)
    amax = np.abs(w).max(1)
    if fmt == "e4m3":
        byte = np.frexp(amax)[1] - 1 + 127 - 7
    else:
        mant, ex = np.frexp(amax / 6.0)
        byte = np.where(mant > 0.5, ex, ex - 1) + 127
    byte = np.clip(np.where(amax > 0, byte, 1), 1, 254)
    scaled = (w * np.exp2(127.0 - byte)[:, None, :]).reshape(k, n).astype(np.float32)
    by_word = np.ascontiguousarray(scaled.reshape(k // 512, 128, 4, n).transpose(0, 1, 3, 2))
    if fmt == "e4m3":
        words = by_word.astype(ml_dtypes.float8_e4m3fn).view(np.uint8)
    else:
        c = by_word.astype(ml_dtypes.float4_e2m1fn).view(np.uint8) & 0xF
        words = (c[..., 0::2] | (c[..., 1::2] << 4)).reshape(k // 512, 128, 2 * n)
    return np.ascontiguousarray(words), np.ascontiguousarray(byte.astype(np.uint8).reshape(k // 512, 16, n))


def unpack_weight(words, scales, fmt):
    g, _, n = scales.shape
    words = np.ascontiguousarray(words).reshape(g, 128, n, -1)
    if fmt == "e4m3":
        vals = words.view(ml_dtypes.float8_e4m3fn).astype(np.float64)
    else:
        nib = np.empty((g, 128, n, 4), np.uint8)
        nib[..., 0::2] = words & 0xF
        nib[..., 1::2] = words >> 4
        vals = E2M1[nib]
    vals = vals * np.repeat(np.exp2(scales.astype(np.float64) - 127.0), 8, axis=1)[..., None]
    return vals.transpose(0, 1, 3, 2).reshape(g * 512, n)


D, T, I, Q = 512, 1024, 512, 128


def setup_inputs():
    n = np.random.standard_normal
    idx = np.stack([np.random.permutation(T)[:I] for _ in range(8)])
    idx2 = np.stack([np.random.permutation(T)[:I] for _ in range(8)])
    idx3 = np.stack([np.random.permutation(T)[:I] for _ in range(8)])
    idx4 = np.stack([np.random.permutation(T)[:I] for _ in range(8)])
    fd = mx_kscale(D)
    keysp = pack_weight(n((D, T)) / fd[:, None], "e2m1")
    return {
        "query": (n((D, Q)) * 1.0 / np.sqrt(D) * fd[:, None]).astype(np.float32),
        "keys_words": keysp[0],
        "keys_scales": keysp[1],
        "lam": (np.random.uniform(0.3, 0.9, (Q, 1))).astype(np.float32),
        "old": (1.0 * n((Q, T))).astype(np.float32),
        "offs": striped8(idx),
        "offs2": striped8(idx2),
        "offs3": striped8(idx3),
        "offs4": striped8(idx4),
    }


def reference(query, keys_words, keys_scales, lam, old, offs, offs2, offs3, offs4):
    idx = unstriped8(offs)
    idx2 = unstriped8(offs2)
    idx3 = unstriped8(offs3)
    idx4 = unstriped8(offs4)
    keysu = unpack_weight(keys_words, keys_scales, "e2m1")
    queryq = mxq(f64(query), 0, "e4m3")
    a = queryq.T @ keysu
    rv = np.log(np.exp(pick8(a, idx2, 16)) + np.exp(pick8(a, idx3, 16)))
    w = pick8(a, idx, 16) - rv * f64(lam)
    f1 = np.zeros((Q, T))
    f1[np.arange(Q)[:, None], idx4[np.arange(Q) % 128 // 16]] = w
    y = f64(old) + f1
    return y

@@ -1,0 +1,132 @@
+from contextlib import ExitStack
+
+import concourse.mybir as mybir
+
+D, T, SLOTS, Q = 512, 1024, 512, 128
+FLOPS = 2 * D * T * Q
+
+F32 = mybir.dt.float32
+BF16 = mybir.dt.bfloat16
+I32 = mybir.dt.int32
+U32 = mybir.dt.uint32
+U16 = mybir.dt.uint16
+U8 = mybir.dt.uint8
+FP8X4 = mybir.dt.float8_e4m3fn_x4
+FP4X4 = mybir.dt.float4_e2m1fn_x4
+ALU = mybir.AluOpType
+ACT = mybir.ActivationFunctionType
+
+P = 128
+PACK = 4
+BANK_WIDTHS = (256, 256, 256, 128, 128)
+HALF = SLOTS // 2
+N_OUT = 256
+
+
+def tile_attend_tworivals_lean_putold_heads_kernel(tc, query, keys_words, keys_scales, lam, old, offs, offs2, offs3, offs4, out):
+    nc = tc.nc
+    with ExitStack() as ctx:
+        lists = ctx.enter_context(tc.tile_pool(name="lists", bufs=1))
+        pool = ctx.enter_context(tc.tile_pool(name="pool", bufs=1))
+        psum = ctx.enter_context(tc.psum_pool(name="psum", bufs=1))
+
+        q_raw = pool.tile([P, PACK, Q], F32, name="q_raw")
+        nc.sync.dma_start(out=q_raw[:], in_=query.rearrange("(p j) q -> p j q", j=PACK))
+
+        k_scale = pool.tile([P, T], U8, name="k_scale", align_bytes=64)
+        for quad in range(4):
+            nc.scalar.dma_start(
+                out=k_scale[32 * quad : 32 * quad + 4, :].bitcast(I32),
+                in_=keys_scales[0, 4 * quad : 4 * quad + 4, :].bitcast(I32),
+            )
+        k_words = pool.tile([P, 2 * T], U8, name="k_words", align_bytes=64)
+        nc.sync.dma_start(out=k_words[:].bitcast(I32), in_=keys_words[0].bitcast(I32))
+
+        o3 = lists.tile([P, SLOTS // 16], U16, name="o3")
+        nc.sync.dma_start(o3[:], offs3)
+        o2 = lists.tile([P, SLOTS // 16], U16, name="o2")
+        nc.sync.dma_start(o2[:], offs2)
+        o1 = lists.tile([P, SLOTS // 16], U16, name="o1")
+        nc.sync.dma_start(o1[:], offs)
+        o4 = lists.tile([P, SLOTS // 16], U16, name="o4")
+        nc.sync.dma_start(o4[:], offs4)
+        old_sb = pool.tile([P, T], F32, name="old_sb")
+        nc.sync.dma_start(out=old_sb[:], in_=old)
+
+        lam_sb = pool.tile([P, 1], F32, name="lam_sb")
+        nc.gpsimd.dma_start(out=lam_sb[:], in_=lam)
+        half = pool.tile([P, 1], F32, name="half")
+        nc.gpsimd.memset(half[:], 0.5)
+        placed = pool.tile([P, T], F32, name="placed")
+        nc.vector.memset(placed[:], 0.0)
+        neg_lam = pool.tile([P, 1], F32, name="neg_lam")
+        nc.scalar.activation(neg_lam[:], lam_sb[:], ACT.Copy, scale=-1.0)
+
+        q_bf = pool.tile([P, Q, PACK], BF16, name="q_bf", align_bytes=64)
+        nc.vector.tensor_copy(out=q_bf[:], in_=q_raw[:].rearrange("p j q -> p q j"))
+        q_codes = pool.tile([P, Q], U32, name="q_codes", align_bytes=64)
+        q_scale = pool.tile([P, Q], U8, name="q_scale", align_bytes=64)
+        nc.vector.quantize_mx(out=q_codes[:].bitcast(FP8X4), scales=q_scale[:], in_=q_bf[:].rearrange("p q j -> p (q j)"))
+
+        a = pool.tile([P, T], F32, name="a")
+        start = 0
+        for b, width in enumerate(BANK_WIDTHS):
+            cols = slice(start, start + width)
+            acc = psum.tile([P, width], F32, name="acc%d" % b)
+            nc.tensor.matmul_mx(
+                out=acc[:],
+                lhsT=q_codes[:].bitcast(FP8X4),
+                lhsT_scale=q_scale[:],
+                rhs=k_words[:, 2 * start : 2 * (start + width)].bitcast(FP4X4),
+                rhs_scale=k_scale[:, cols],
+                start=True,
+                stop=True,
+            )
+            if b % 2 == 0:
+                nc.scalar.copy(a[:, cols], acc[:])
+            else:
+                nc.vector.tensor_copy(a[:, cols], acc[:])
+            start = start + width
+
+        lo, hi = slice(0, HALF), slice(HALF, SLOTS)
+        lo_l, hi_l = slice(0, HALF // 16), slice(HALF // 16, SLOTS // 16)
+
+        y = pool.tile([P, SLOTS], F32, name="y")
+        x_hi = pool.tile([P, HALF], F32, name="x_hi", tag="x_then_z")
+        d_lo = pool.tile([P, HALF], F32, name="d_lo")
+        d_hi = pool.tile([P, HALF], F32, name="d_hi", tag="d_then_log")
+        tau = pool.tile([P, SLOTS], F32, name="tau")
+        nc.scalar.activation(y[:, lo], a[:].indirect(o3[:, lo_l]), ACT.Copy)
+        nc.vector.tensor_copy(x_hi[:], a[:].indirect(o2[:, hi_l]))
+        nc.scalar.activation(y[:, hi], a[:].indirect(o3[:, hi_l]), ACT.Copy)
+        nc.vector.tensor_tensor(d_lo[:], a[:].indirect(o2[:, lo_l]), y[:, lo], ALU.subtract)
+        nc.vector.tensor_tensor(d_hi[:], x_hi[:], y[:, hi], ALU.subtract)
+        nc.scalar.activation(tau[:, lo], d_lo[:], ACT.Tanh, scale=0.5)
+        nc.scalar.activation(tau[:, hi], d_hi[:], ACT.Tanh, scale=0.5)
+
+        top = pool.tile([P, SLOTS], F32, name="top")
+        mag = pool.tile([P, SLOTS], F32, name="mag")
+        nc.vector.tensor_tensor(top[:, hi], x_hi[:], y[:, hi], ALU.max)
+        nc.vector.scalar_tensor_tensor(mag[:, lo], tau[:, lo], -1.0, tau[:, lo], ALU.mult, ALU.max)
+        nc.vector.scalar_tensor_tensor(top[:, lo], d_lo[:], 0.0, y[:, lo], ALU.max, ALU.add)
+        nc.vector.scalar_tensor_tensor(mag[:, hi], tau[:, hi], -1.0, tau[:, hi], ALU.mult, ALU.max)
+        z = pool.tile([P, SLOTS], F32, name="z", tag="x_then_z")
+        nc.vector.tensor_copy(z[:], a[:].indirect(o1[:]))
+        base = pool.tile([P, SLOTS], F32, name="base")
+        nc.vector.scalar_tensor_tensor(base[:], top[:], neg_lam[:], z[:], ALU.mult, ALU.add)
+
+        log_lo = pool.tile([P, HALF], F32, name="log_lo", tag="d_then_log")
+        log_hi = pool.tile([P, HALF], F32, name="log_hi")
+        term = pool.tile([P, SLOTS], F32, name="term")
+        nc.scalar.activation(log_lo[:], mag[:, lo], ACT.Ln, bias=half[:], scale=0.5)
+        nc.scalar.activation(log_hi[:], mag[:, hi], ACT.Ln, bias=half[:], scale=0.5)
+        nc.scalar.activation(term[:, lo], log_lo[:], ACT.Identity, scale=lam_sb[:])
+        nc.vector.tensor_scalar(term[:, hi], log_hi[:], lam_sb[:], None, ALU.mult)
+        nc.vector.tensor_tensor(placed[:].indirect(o4[:]), base[:], term[:], ALU.add)
+
+        res = pool.tile([P, T], F32, name="res")
+        for c in range(T // N_OUT):
+            cols = slice(c * N_OUT, (c + 1) * N_OUT)
+            nc.vector.tensor_tensor(res[:, cols], placed[:, cols], old_sb[:, cols], ALU.add)
+            eng = nc.sync if c % 2 == 0 else nc.scalar
+            eng.dma_start(out=out[:, cols], in_=res[:, cols])

@@ -20,7 +20,8 @@ P = 128
 PACK = 4
 BANK_WIDTHS = (256, 256, 256, 128, 128)
 HALF = SLOTS // 2
-N_OUT = 256
+OUT_WIDTHS = (128, 256, 256, 256, 128)
+LOG_SPLIT = 384
 
 
 def tile_attend_tworivals_lean_putold_heads_kernel(tc, query, keys_words, keys_scales, lam, old, offs, offs2, offs3, offs4, out):
@@ -48,19 +49,17 @@ def tile_attend_tworivals_lean_putold_heads_kernel(tc, query, keys_words, keys_s
         nc.sync.dma_start(o2[:], offs2)
         o1 = lists.tile([P, SLOTS // 16], U16, name="o1")
         nc.sync.dma_start(o1[:], offs)
+        lam_sb = pool.tile([P, 1], F32, name="lam_sb")
+        nc.sync.dma_start(out=lam_sb[:], in_=lam)
         o4 = lists.tile([P, SLOTS // 16], U16, name="o4")
         nc.sync.dma_start(o4[:], offs4)
         old_sb = pool.tile([P, T], F32, name="old_sb")
         nc.sync.dma_start(out=old_sb[:], in_=old)
 
-        lam_sb = pool.tile([P, 1], F32, name="lam_sb")
-        nc.gpsimd.dma_start(out=lam_sb[:], in_=lam)
         half = pool.tile([P, 1], F32, name="half")
         nc.gpsimd.memset(half[:], 0.5)
         placed = pool.tile([P, T], F32, name="placed")
         nc.vector.memset(placed[:], 0.0)
-        neg_lam = pool.tile([P, 1], F32, name="neg_lam")
-        nc.scalar.activation(neg_lam[:], lam_sb[:], ACT.Copy, scale=-1.0)
 
         q_bf = pool.tile([P, Q, PACK], BF16, name="q_bf", align_bytes=64)
         nc.vector.tensor_copy(out=q_bf[:], in_=q_raw[:].rearrange("p j q -> p q j"))
@@ -91,42 +90,44 @@ def tile_attend_tworivals_lean_putold_heads_kernel(tc, query, keys_words, keys_s
         lo, hi = slice(0, HALF), slice(HALF, SLOTS)
         lo_l, hi_l = slice(0, HALF // 16), slice(HALF // 16, SLOTS // 16)
 
-        y = pool.tile([P, SLOTS], F32, name="y")
-        x_hi = pool.tile([P, HALF], F32, name="x_hi", tag="x_then_z")
+        x = pool.tile([P, SLOTS], F32, name="x")
+        ny = pool.tile([P, SLOTS], F32, name="ny", tag="y_then_z")
         d_lo = pool.tile([P, HALF], F32, name="d_lo")
         d_hi = pool.tile([P, HALF], F32, name="d_hi", tag="d_then_log")
+        z_lo = pool.tile([P, HALF], F32, name="z_lo")
         tau = pool.tile([P, SLOTS], F32, name="tau")
-        nc.scalar.activation(y[:, lo], a[:].indirect(o3[:, lo_l]), ACT.Copy)
-        nc.vector.tensor_copy(x_hi[:], a[:].indirect(o2[:, hi_l]))
-        nc.scalar.activation(y[:, hi], a[:].indirect(o3[:, hi_l]), ACT.Copy)
-        nc.vector.tensor_tensor(d_lo[:], a[:].indirect(o2[:, lo_l]), y[:, lo], ALU.subtract)
-        nc.vector.tensor_tensor(d_hi[:], x_hi[:], y[:, hi], ALU.subtract)
-        nc.scalar.activation(tau[:, lo], d_lo[:], ACT.Tanh, scale=0.5)
-        nc.scalar.activation(tau[:, hi], d_hi[:], ACT.Tanh, scale=0.5)
+        for s, sl in ((lo, lo_l), (hi, hi_l)):
+            nc.scalar.activation(ny[:, s], a[:].indirect(o3[:, sl]), ACT.Copy, scale=-1.0)
+            nc.vector.tensor_copy(x[:, s], a[:].indirect(o2[:, sl]))
+        nc.scalar.activation(z_lo[:], a[:].indirect(o1[:, lo_l]), ACT.Copy)
+        for s, d in ((lo, d_lo), (hi, d_hi)):
+            nc.vector.tensor_tensor(d[:], x[:, s], ny[:, s], ALU.add)
+            nc.scalar.activation(tau[:, s], d[:], ACT.Tanh, scale=0.5)
+        ln_half = pool.tile([P, 1], F32, name="ln_half", tag="d_then_log")
+        nc.scalar.activation(ln_half[:], half[:], ACT.Ln)
 
-        top = pool.tile([P, SLOTS], F32, name="top")
+        neg_top = pool.tile([P, SLOTS], F32, name="neg_top")
         mag = pool.tile([P, SLOTS], F32, name="mag")
-        nc.vector.tensor_tensor(top[:, hi], x_hi[:], y[:, hi], ALU.max)
-        nc.vector.scalar_tensor_tensor(mag[:, lo], tau[:, lo], -1.0, tau[:, lo], ALU.mult, ALU.max)
-        nc.vector.scalar_tensor_tensor(top[:, lo], d_lo[:], 0.0, y[:, lo], ALU.max, ALU.add)
-        nc.vector.scalar_tensor_tensor(mag[:, hi], tau[:, hi], -1.0, tau[:, hi], ALU.mult, ALU.max)
-        z = pool.tile([P, SLOTS], F32, name="z", tag="x_then_z")
-        nc.vector.tensor_copy(z[:], a[:].indirect(o1[:]))
         base = pool.tile([P, SLOTS], F32, name="base")
-        nc.vector.scalar_tensor_tensor(base[:], top[:], neg_lam[:], z[:], ALU.mult, ALU.add)
+        nc.vector.scalar_tensor_tensor(neg_top[:], x[:], -1.0, ny[:], ALU.mult, ALU.min)
+        z_hi = pool.tile([P, HALF], F32, name="z_hi", tag="y_then_z")
+        nc.vector.tensor_copy(z_hi[:], a[:].indirect(o1[:, hi_l]))
+        nc.vector.scalar_tensor_tensor(mag[:], tau[:], -1.0, tau[:], ALU.mult, ALU.max)
+        for s, z in ((lo, z_lo), (hi, z_hi)):
+            nc.vector.scalar_tensor_tensor(base[:, s], neg_top[:, s], lam_sb[:], z[:], ALU.mult, ALU.add)
 
-        log_lo = pool.tile([P, HALF], F32, name="log_lo", tag="d_then_log")
-        log_hi = pool.tile([P, HALF], F32, name="log_hi")
+        logs = pool.tile([P, SLOTS], F32, name="logs")
         term = pool.tile([P, SLOTS], F32, name="term")
-        nc.scalar.activation(log_lo[:], mag[:, lo], ACT.Ln, bias=half[:], scale=0.5)
-        nc.scalar.activation(log_hi[:], mag[:, hi], ACT.Ln, bias=half[:], scale=0.5)
-        nc.scalar.activation(term[:, lo], log_lo[:], ACT.Identity, scale=lam_sb[:])
-        nc.vector.tensor_scalar(term[:, hi], log_hi[:], lam_sb[:], None, ALU.mult)
+        for s in (slice(0, LOG_SPLIT), slice(LOG_SPLIT, SLOTS)):
+            nc.scalar.activation(logs[:, s], mag[:, s], ACT.Ln, bias=1.0)
+            nc.vector.tensor_scalar(term[:, s], logs[:, s], ln_half[:], lam_sb[:], ALU.add, ALU.mult)
         nc.vector.tensor_tensor(placed[:].indirect(o4[:]), base[:], term[:], ALU.add)
 
         res = pool.tile([P, T], F32, name="res")
-        for c in range(T // N_OUT):
-            cols = slice(c * N_OUT, (c + 1) * N_OUT)
+        start = 0
+        for c, width in enumerate(OUT_WIDTHS):
+            cols = slice(start, start + width)
             nc.vector.tensor_tensor(res[:, cols], placed[:, cols], old_sb[:, cols], ALU.add)
             eng = nc.sync if c % 2 == 0 else nc.scalar
             eng.dma_start(out=out[:, cols], in_=res[:, cols])
+            start = start + width

@@ -22,6 +22,7 @@ BANK_WIDTHS = (256, 256, 256, 128, 128)
 HALF = SLOTS // 2
 OUT_WIDTHS = (128, 256, 256, 256, 128)
 LOG_SPLIT = 384
+PIECE = 128
 
 
 def tile_attend_tworivals_lean_putold_heads_kernel(tc, query, keys_words, keys_scales, lam, old, offs, offs2, offs3, offs4, out):
@@ -91,16 +92,14 @@ def tile_attend_tworivals_lean_putold_heads_kernel(tc, query, keys_words, keys_s
         lo_l, hi_l = slice(0, HALF // 16), slice(HALF // 16, SLOTS // 16)
 
         x = pool.tile([P, SLOTS], F32, name="x")
-        ny = pool.tile([P, SLOTS], F32, name="ny", tag="y_then_z")
-        d_lo = pool.tile([P, HALF], F32, name="d_lo")
-        d_hi = pool.tile([P, HALF], F32, name="d_hi", tag="d_then_log")
-        z_lo = pool.tile([P, HALF], F32, name="z_lo")
+        ny = pool.tile([P, SLOTS], F32, name="ny")
         tau = pool.tile([P, SLOTS], F32, name="tau")
         for s, sl in ((lo, lo_l), (hi, hi_l)):
             nc.scalar.activation(ny[:, s], a[:].indirect(o3[:, sl]), ACT.Copy, scale=-1.0)
             nc.vector.tensor_copy(x[:, s], a[:].indirect(o2[:, sl]))
-        nc.scalar.activation(z_lo[:], a[:].indirect(o1[:, lo_l]), ACT.Copy)
-        for s, d in ((lo, d_lo), (hi, d_hi)):
+        for i, tag in enumerate(("d_first", "d_then_z", "d_third", "d_then_log")):
+            s = slice(i * PIECE, (i + 1) * PIECE)
+            d = pool.tile([P, PIECE], F32, name="d%d" % i, tag=tag)
             nc.vector.tensor_tensor(d[:], x[:, s], ny[:, s], ALU.add)
             nc.scalar.activation(tau[:, s], d[:], ACT.Tanh, scale=0.5)
         ln_half = pool.tile([P, 1], F32, name="ln_half", tag="d_then_log")
@@ -110,11 +109,13 @@ def tile_attend_tworivals_lean_putold_heads_kernel(tc, query, keys_words, keys_s
         mag = pool.tile([P, SLOTS], F32, name="mag")
         base = pool.tile([P, SLOTS], F32, name="base")
         nc.vector.scalar_tensor_tensor(neg_top[:], x[:], -1.0, ny[:], ALU.mult, ALU.min)
-        z_hi = pool.tile([P, HALF], F32, name="z_hi", tag="y_then_z")
-        nc.vector.tensor_copy(z_hi[:], a[:].indirect(o1[:, hi_l]))
-        nc.vector.scalar_tensor_tensor(mag[:], tau[:], -1.0, tau[:], ALU.mult, ALU.max)
-        for s, z in ((lo, z_lo), (hi, z_hi)):
-            nc.vector.scalar_tensor_tensor(base[:, s], neg_top[:, s], lam_sb[:], z[:], ALU.mult, ALU.add)
+        for s in (lo, hi):
+            nc.vector.scalar_tensor_tensor(mag[:, s], tau[:, s], -1.0, tau[:, s], ALU.mult, ALU.max)
+        z = pool.tile([P, SLOTS], F32, name="z", tag="d_then_z")
+        for s, sl in ((lo, lo_l), (hi, hi_l)):
+            nc.vector.tensor_copy(z[:, s], a[:].indirect(o1[:, sl]))
+        for s in (lo, hi):
+            nc.vector.scalar_tensor_tensor(base[:, s], neg_top[:, s], lam_sb[:], z[:, s], ALU.mult, ALU.add)
 
         logs = pool.tile([P, SLOTS], F32, name="logs")
         term = pool.tile([P, SLOTS], F32, name="term")

from contextlib import ExitStack

import concourse.mybir as mybir

D, T, SLOTS, Q = 512, 1024, 512, 128
FLOPS = 2 * D * T * Q

F32 = mybir.dt.float32
BF16 = mybir.dt.bfloat16
I32 = mybir.dt.int32
U32 = mybir.dt.uint32
U16 = mybir.dt.uint16
U8 = mybir.dt.uint8
FP8X4 = mybir.dt.float8_e4m3fn_x4
FP4X4 = mybir.dt.float4_e2m1fn_x4
ALU = mybir.AluOpType
ACT = mybir.ActivationFunctionType

P = 128
PACK = 4
BANK_WIDTHS = (256, 256, 256, 128, 128)
HALF = SLOTS // 2
OUT_WIDTHS = (128, 256, 256, 256, 128)
LOG_SPLIT = 384
PIECE = 128


def tile_attend_tworivals_lean_putold_heads_kernel(tc, query, keys_words, keys_scales, lam, old, offs, offs2, offs3, offs4, out):
    nc = tc.nc
    with ExitStack() as ctx:
        lists = ctx.enter_context(tc.tile_pool(name="lists", bufs=1))
        pool = ctx.enter_context(tc.tile_pool(name="pool", bufs=1))
        psum = ctx.enter_context(tc.psum_pool(name="psum", bufs=1))

        q_raw = pool.tile([P, PACK, Q], F32, name="q_raw")
        nc.sync.dma_start(out=q_raw[:], in_=query.rearrange("(p j) q -> p j q", j=PACK))

        k_scale = pool.tile([P, T], U8, name="k_scale", align_bytes=64)
        for quad in range(4):
            nc.scalar.dma_start(
                out=k_scale[32 * quad : 32 * quad + 4, :].bitcast(I32),
                in_=keys_scales[0, 4 * quad : 4 * quad + 4, :].bitcast(I32),
            )
        k_words = pool.tile([P, 2 * T], U8, name="k_words", align_bytes=64)
        nc.sync.dma_start(out=k_words[:].bitcast(I32), in_=keys_words[0].bitcast(I32))

        o3 = lists.tile([P, SLOTS // 16], U16, name="o3")
        nc.sync.dma_start(o3[:], offs3)
        o2 = lists.tile([P, SLOTS // 16], U16, name="o2")
        nc.sync.dma_start(o2[:], offs2)
        o1 = lists.tile([P, SLOTS // 16], U16, name="o1")
        nc.sync.dma_start(o1[:], offs)
        lam_sb = pool.tile([P, 1], F32, name="lam_sb")
        nc.sync.dma_start(out=lam_sb[:], in_=lam)
        o4 = lists.tile([P, SLOTS // 16], U16, name="o4")
        nc.sync.dma_start(o4[:], offs4)
        old_sb = pool.tile([P, T], F32, name="old_sb")
        nc.sync.dma_start(out=old_sb[:], in_=old)

        half = pool.tile([P, 1], F32, name="half")
        nc.gpsimd.memset(half[:], 0.5)
        placed = pool.tile([P, T], F32, name="placed")
        nc.vector.memset(placed[:], 0.0)

        q_bf = pool.tile([P, Q, PACK], BF16, name="q_bf", align_bytes=64)
        nc.vector.tensor_copy(out=q_bf[:], in_=q_raw[:].rearrange("p j q -> p q j"))
        q_codes = pool.tile([P, Q], U32, name="q_codes", align_bytes=64)
        q_scale = pool.tile([P, Q], U8, name="q_scale", align_bytes=64)
        nc.vector.quantize_mx(out=q_codes[:].bitcast(FP8X4), scales=q_scale[:], in_=q_bf[:].rearrange("p q j -> p (q j)"))

        a = pool.tile([P, T], F32, name="a")
        start = 0
        for b, width in enumerate(BANK_WIDTHS):
            cols = slice(start, start + width)
            acc = psum.tile([P, width], F32, name="acc%d" % b)
            nc.tensor.matmul_mx(
                out=acc[:],
                lhsT=q_codes[:].bitcast(FP8X4),
                lhsT_scale=q_scale[:],
                rhs=k_words[:, 2 * start : 2 * (start + width)].bitcast(FP4X4),
                rhs_scale=k_scale[:, cols],
                start=True,
                stop=True,
            )
            if b % 2 == 0:
                nc.scalar.copy(a[:, cols], acc[:])
            else:
                nc.vector.tensor_copy(a[:, cols], acc[:])
            start = start + width

        lo, hi = slice(0, HALF), slice(HALF, SLOTS)
        lo_l, hi_l = slice(0, HALF // 16), slice(HALF // 16, SLOTS // 16)

        x = pool.tile([P, SLOTS], F32, name="x")
        ny = pool.tile([P, SLOTS], F32, name="ny")
        tau = pool.tile([P, SLOTS], F32, name="tau")
        for s, sl in ((lo, lo_l), (hi, hi_l)):
            nc.scalar.activation(ny[:, s], a[:].indirect(o3[:, sl]), ACT.Copy, scale=-1.0)
            nc.vector.tensor_copy(x[:, s], a[:].indirect(o2[:, sl]))
        for i, tag in enumerate(("d_first", "d_then_z", "d_third", "d_then_log")):
            s = slice(i * PIECE, (i + 1) * PIECE)
            d = pool.tile([P, PIECE], F32, name="d%d" % i, tag=tag)
            nc.vector.tensor_tensor(d[:], x[:, s], ny[:, s], ALU.add)
            nc.scalar.activation(tau[:, s], d[:], ACT.Tanh, scale=0.5)
        ln_half = pool.tile([P, 1], F32, name="ln_half", tag="d_then_log")
        nc.scalar.activation(ln_half[:], half[:], ACT.Ln)

        neg_top = pool.tile([P, SLOTS], F32, name="neg_top")
        mag = pool.tile([P, SLOTS], F32, name="mag")
        base = pool.tile([P, SLOTS], F32, name="base")
        nc.vector.scalar_tensor_tensor(neg_top[:], x[:], -1.0, ny[:], ALU.mult, ALU.min)
        for s in (lo, hi):
            nc.vector.scalar_tensor_tensor(mag[:, s], tau[:, s], -1.0, tau[:, s], ALU.mult, ALU.max)
        z = pool.tile([P, SLOTS], F32, name="z", tag="d_then_z")
        for s, sl in ((lo, lo_l), (hi, hi_l)):
            nc.vector.tensor_copy(z[:, s], a[:].indirect(o1[:, sl]))
        for s in (lo, hi):
            nc.vector.scalar_tensor_tensor(base[:, s], neg_top[:, s], lam_sb[:], z[:, s], ALU.mult, ALU.add)

        logs = pool.tile([P, SLOTS], F32, name="logs")
        term = pool.tile([P, SLOTS], F32, name="term")
        for s in (slice(0, LOG_SPLIT), slice(LOG_SPLIT, SLOTS)):
            nc.scalar.activation(logs[:, s], mag[:, s], ACT.Ln, bias=1.0)
            nc.vector.tensor_scalar(term[:, s], logs[:, s], ln_half[:], lam_sb[:], ALU.add, ALU.mult)
        nc.vector.tensor_tensor(placed[:].indirect(o4[:]), base[:], term[:], ALU.add)

        res = pool.tile([P, T], F32, name="res")
        start = 0
        for c, width in enumerate(OUT_WIDTHS):
            cols = slice(start, start + width)
            nc.vector.tensor_tensor(res[:, cols], placed[:, cols], old_sb[:, cols], ALU.add)
            eng = nc.sync if c % 2 == 0 else nc.scalar
            eng.dma_start(out=out[:, cols], in_=res[:, cols])
            start = start + width
